import numpy as np
import ml_dtypes


def mxq(x, axis, fmt="e4m3"):
    dtype, down = {"e4m3": (ml_dtypes.float8_e4m3fn, 7), "e5m2": (ml_dtypes.float8_e5m2, 14)}[fmt]
    v = np.moveaxis(np.asarray(x, np.float32).astype(ml_dtypes.bfloat16).astype(np.float64), axis, -1)
    blocks = v.reshape(v.shape[:-1] + (-1, 32))
    amax = np.abs(blocks).max(-1, keepdims=True)
    byte = np.maximum(np.where(amax > 0, np.frexp(amax)[1] - 1 + 127, 0) - down, 1)
    scale = np.exp2(byte - 127.0)
    codes = (blocks / scale).astype(np.float32).astype(dtype).astype(np.float64)
    return np.moveaxis((codes * scale).reshape(v.shape), -1, axis)


WIDE = False


def mx_kscale(k):
    if not WIDE:
        return np.ones(k)
    levels = np.array([10, -10, 5, -5, 0])
    if k % 512:
        return np.exp2(np.random.permutation(np.resize(levels, k // 32))).repeat(32)
    a = np.empty((k // 512, 16))
    for p in range(k // 512):
        a[p, :8] = np.random.permutation(np.resize(levels, 8))
        for g in range(8):
            far = levels[np.abs(levels - a[p, g]) >= 10]
            a[p, g + 8] = far[np.random.randint(len(far))]
    return np.exp2(a.ravel()).repeat(32)


def f64(x):
    return np.asarray(x).astype(np.float64)


def striped(idx):
    return np.tile(idx.reshape(-1, 16).T, (8, 1)).astype(np.uint16)


def unstriped(offs):
    return offs[:16].T.reshape(-1).astype(np.int64)


def striped8(idx):
    return np.concatenate([v.reshape(-1, 16).T for v in idx]).astype(np.uint16)


def unstriped8(offs):
    return np.stack([offs[16 * g:16 * g + 16].T.reshape(-1) for g in range(8)]).astype(np.int64)


E2M1 = np.array([0.0, 0.5, 1.0, 1.5, 2.0, 3.0, 4.0, 6.0, -0.0, -0.5, -1.0, -1.5, -2.0, -3.0, -4.0, -6.0])


def pack_weight(w, fmt):
    k, n = w.shape
    w = f64(np.asarray(w, np.float32).astype(ml_dtypes.bfloat16)).reshape(k // 32, 32, n)
    amax = np.abs(w).max(1)
    if fmt == "e4m3":
        byte = np.frexp(amax)[1] - 1 + 127 - 7
    else:
        mant, ex = np.frexp(amax / 6.0)
        byte = np.where(mant > 0.5, ex, ex - 1) + 127
    byte = np.clip(np.where(amax > 0, byte, 1), 1, 254)
    scaled = (w * np.exp2(127.0 - byte)[:, None, :]).reshape(k, n).astype(np.float32)
    by_word = np.ascontiguousarray(scaled.reshape(k // 512, 128, 4, n).transpose(0, 1, 3, 2))
    if fmt == "e4m3":
        words = by_word.astype(ml_dtypes.float8_e4m3fn).view(np.uint8)
    else:
        c = by_word.astype(ml_dtypes.float4_e2m1fn).view(np.uint8) & 0xF
        words = (c[..., 0::2] | (c[..., 1::2] << 4)).reshape(k // 512, 128, 2 * n)
    return np.ascontiguousarray(words), np.ascontiguousarray(byte.astype(np.uint8).reshape(k // 512, 16, n))


def unpack_weight(words, scales, fmt):
    g, _, n = scales.shape
    words = np.ascontiguousarray(words).reshape(g, 128, n, -1)
    if fmt == "e4m3":
        vals = words.view(ml_dtypes.float8_e4m3fn).astype(np.float64)
    else:
        nib = np.empty((g, 128, n, 4), np.uint8)
        nib[..., 0::2] = words & 0xF
        nib[..., 1::2] = words >> 4
        vals = E2M1[nib]
    vals = vals * np.repeat(np.exp2(scales.astype(np.float64) - 127.0), 8, axis=1)[..., None]
    return vals.transpose(0, 1, 3, 2).reshape(g * 512, n)


def pack_table(v):
    words, scales = pack_weight(v, "e4m3")
    return np.concatenate([words.reshape(words.shape[0], -1), scales.reshape(scales.shape[0], -1)], axis=1)


def unpack_table(tab):
    g, t = tab.shape[0], tab.shape[1] // 528
    return unpack_weight(tab[:, :512 * t].reshape(g, 128, t, 4), tab[:, 512 * t:].reshape(g, 16, t), "e4m3")


K, M, T, S = 512, 512, 4096, 2048


def setup_inputs():
    n = np.random.standard_normal
    s = mx_kscale(K)[:, None]
    u = mx_kscale(512)[:, None]
    p_w2 = pack_weight(1.4 * n((512, M)) / np.sqrt(512) / u, "e2m1")
    return {
        "tab": pack_table(n((K, T)) * s),
        "w1": (n((K, 512)) / np.sqrt(K) / s * u.T).astype(np.float32),
        "w2_words": p_w2[0],
        "w2_scales": p_w2[1],
        "wgo": np.repeat(np.random.uniform(0.5, 2.0, (8, S)), 16, axis=0).astype(np.float32),
        "offs": striped(np.random.permutation(T)[:S]),
        "offs2": striped8(np.stack([np.random.permutation(T)[:S] for _ in range(8)])),
    }


def reference(tab, w1, w2_words, w2_scales, wgo, offs, offs2):
    tab_ = unpack_table(tab)[:, unstriped(offs)]
    w1_ = mxq(f64(w1), 0, "e4m3")
    w2_ = unpack_weight(w2_words, w2_scales, "e2m1")
    h_ = mxq(np.maximum(w1_.T @ tab_, 0.0), 0, "e4m3")
    y = w2_.T @ h_
    place = unstriped8(offs2)[np.arange(M) % 128 // 16]
    out = np.zeros((M, T))
    out[np.arange(M)[:, None], place] = f64(wgo)[np.arange(M) % 128] * (y)
    return out

@@ -1,0 +1,158 @@
+from contextlib import ExitStack
+
+import concourse.mybir as mybir
+
+K, M, T, S = 512, 512, 4096, 2048
+FLOPS = 2 * S * (K * 512 + 512 * M)
+
+F32 = mybir.dt.float32
+BF16 = mybir.dt.bfloat16
+I32 = mybir.dt.int32
+U32 = mybir.dt.uint32
+U16 = mybir.dt.uint16
+U8 = mybir.dt.uint8
+FP8X4 = mybir.dt.float8_e4m3fn_x4
+FP4X4 = mybir.dt.float4_e2m1fn_x4
+RELU = mybir.ActivationFunctionType.Relu
+MULT = mybir.AluOpType.mult
+
+P = 128
+PACK = 4
+GROUP = 16
+BANK = 512
+GATHERS = [512,512,1024]
+PIECES = [256,256,256,256,256,256,512]
+AHEAD = 2
+
+
+def starts(widths):
+    return [sum(widths[:i]) for i in range(len(widths))]
+
+
+def tile_list_tabhs_m_none_kernel(tc, tab, w1, w2_words, w2_scales, wgo, offs, offs2, out):
+    nc = tc.nc
+    with ExitStack() as ctx:
+        keep = ctx.enter_context(tc.tile_pool(name="keep", bufs=1))
+        ypool = ctx.enter_context(tc.tile_pool(name="ypool", bufs=2))
+        hpsum = ctx.enter_context(tc.psum_pool(name="hpsum", bufs=5))
+        ypsum = ctx.enter_context(tc.psum_pool(name="ypsum", bufs=3))
+
+        pick = keep.tile([P, S // GROUP], U16, name="pick")
+        place = keep.tile([P, S // GROUP], U16, name="place")
+        tab_words = keep.tile([P, T], I32, name="tab_words", align_bytes=64)
+        tab_scales = keep.tile([P, T], U8, name="tab_scales", align_bytes=64)
+        w1_raw = keep.tile([P, PACK, 512], F32, name="w1_raw", tag="w1_raw_then_wgo", align_bytes=64)
+        w2_plane = keep.tile([P, M], U8, name="w2_plane", align_bytes=64)
+        warm_in = keep.tile([P, 1], F32, name="warm_in")
+        warm_out = keep.tile([P, 1], F32, name="warm_out")
+        page_a = keep.tile([P, T], F32, name="page_a", align_bytes=64)
+
+        nc.vector.memset(tab_scales[:].bitcast(I32), 0)
+        nc.vector.memset(warm_in[:], 0.0)
+        nc.vector.memset(w2_plane[:].bitcast(I32), 0)
+        nc.vector.memset(page_a[:], 0.0)
+
+        nc.sync.dma_start(pick[:], offs)
+        nc.sync.dma_start(w1_raw[:], w1.rearrange("(p j) c -> p j c", j=PACK))
+        nc.sync.dma_start(tab_words[:], tab[0, 0 : K * T].rearrange("(p b) -> p b", p=P).bitcast(I32))
+        nc.sync.dma_start(place[:], offs2)
+        scale_rows = tab[0, K * T : K * T + 16 * T].rearrange("(q b) -> q b", q=16).bitcast(I32)
+        for q in range(4):
+            nc.scalar.dma_start(tab_scales[32 * q : 32 * q + 4, :].bitcast(I32), scale_rows[4 * q : 4 * q + 4, :])
+        nc.scalar.activation(warm_out[:], warm_in[:], RELU)
+        w2_rows = w2_scales[0].bitcast(I32)
+        for q in range(4):
+            nc.sync.dma_start(w2_plane[32 * q : 32 * q + 4, :].bitcast(I32), w2_rows[4 * q : 4 * q + 4, :])
+
+        v_scales = keep.tile([P, S], U8, name="v_scales", align_bytes=64)
+        nc.vector.tensor_copy(v_scales[:], tab_scales[:].indirect(pick[:]))
+
+        w1_bf = keep.tile([P, 512 * PACK], BF16, name="w1_bf", tag="w1_bf_then_w2", align_bytes=64)
+        nc.scalar.copy(
+            w1_bf[:].rearrange("p (t m j) -> p m j t", t=PACK, j=PACK),
+            w1_raw[:].rearrange("p j (m t) -> p m j t", t=PACK),
+        )
+        w1_codes = keep.tile([P, 512], U32, name="w1_codes", align_bytes=64)
+        w1_plane = keep.tile([P, 512], U8, name="w1_plane", align_bytes=64)
+        nc.vector.quantize_mx(out=w1_codes[:].bitcast(FP8X4), scales=w1_plane[:], in_=w1_bf[:])
+
+        gate = keep.tile([P, S], F32, name="gate", tag="w1_raw_then_wgo", align_bytes=64)
+        nc.sync.dma_start(gate[:], wgo)
+        w2_codes = keep.tile([P, 2 * M], U8, name="w2_codes", tag="w1_bf_then_w2", align_bytes=64)
+        nc.sync.dma_start(w2_codes[:].bitcast(I32), w2_words[0].bitcast(I32))
+
+        v_words = keep.tile([P, S], U32, name="v_words", align_bytes=64)
+        for j0, n in zip(starts(GATHERS), GATHERS):
+            nc.vector.tensor_copy(
+                v_words[:, j0 : j0 + n],
+                tab_words[:].bitcast(U32).indirect(pick[:, j0 // GROUP : (j0 + n) // GROUP]),
+            )
+
+        h_bf = keep.tile([P, S * PACK], BF16, name="h_bf", tag="h_bf_then_page", align_bytes=64)
+        h_codes = keep.tile([P, S], U32, name="h_codes", align_bytes=64)
+        h_plane = keep.tile([P, S], U8, name="h_plane", align_bytes=64)
+
+        def hidden(j0, n):
+            for c0 in range(j0, j0 + n, P):
+                bank = hpsum.tile([P, PACK, P], F32, name="h_bank")
+                for t in range(PACK):
+                    nc.tensor.matmul_mx(
+                        out=bank[:, t, :],
+                        lhsT=w1_codes[:, t * P : (t + 1) * P].bitcast(FP8X4),
+                        lhsT_scale=w1_plane[:, t * P : (t + 1) * P],
+                        rhs=v_words[:, c0 : c0 + P].bitcast(FP8X4),
+                        rhs_scale=v_scales[:, c0 : c0 + P],
+                        start=True,
+                        stop=True,
+                    )
+                nc.scalar.activation(
+                    h_bf[:, c0 * PACK : (c0 + P) * PACK].rearrange("p (n t) -> p n t", t=PACK),
+                    bank[:].rearrange("p t n -> p n t"),
+                    RELU,
+                )
+            nc.vector.quantize_mx(
+                out=h_codes[:, j0 : j0 + n].bitcast(FP8X4),
+                scales=h_plane[:, j0 : j0 + n],
+                in_=h_bf[:, j0 * PACK : (j0 + n) * PACK],
+            )
+
+        def project(m, y, j0, n):
+            bank = ypsum.tile([P, BANK], F32, name="y_bank")
+            nc.tensor.matmul_mx(
+                out=bank[:, 0:n],
+                lhsT=w2_codes[:, 2 * m * P : 2 * (m + 1) * P].bitcast(FP4X4),
+                lhsT_scale=w2_plane[:, m * P : (m + 1) * P],
+                rhs=h_codes[:, j0 : j0 + n].bitcast(FP8X4),
+                rhs_scale=h_plane[:, j0 : j0 + n],
+                start=True,
+                stop=True,
+            )
+            nc.scalar.copy(y[:, j0 : j0 + n], bank[:, 0:n])
+
+        def scatter(page, y, j0, n):
+            nc.vector.tensor_tensor(
+                page[:].indirect(place[:, j0 // GROUP : (j0 + n) // GROUP]),
+                y[:, j0 : j0 + n],
+                gate[:, j0 : j0 + n],
+                MULT,
+            )
+
+        pieces = list(zip(starts(PIECES), PIECES))
+        y0 = ypool.tile([P, S], F32, name="y")
+        for i in range(len(pieces) + AHEAD):
+            if i < len(pieces):
+                hidden(*pieces[i])
+            if i >= AHEAD:
+                project(0, y0, *pieces[i - AHEAD])
+                scatter(page_a, y0, *pieces[i - AHEAD])
+        nc.sync.dma_start(out[0:P, :], page_a[:])
+
+        page_b = keep.tile([P, T], F32, name="page_b", tag="h_bf_then_page", align_bytes=64)
+        nc.gpsimd.memset(page_b[:], 0.0)
+        for m in range(1, M // P):
+            page = page_b if m % 2 else page_a
+            y = ypool.tile([P, S], F32, name="y")
+            for j0 in range(0, S, BANK):
+                project(m, y, j0, BANK)
+            scatter(page, y, 0, S)
+            nc.sync.dma_start(out[m * P : (m + 1) * P, :], page[:])

@@ -39,27 +39,33 @@ def tile_list_tabhs_m_none_kernel(tc, tab, w1, w2_words, w2_scales, wgo, offs, o
 
         pick = keep.tile([P, S // GROUP], U16, name="pick")
         place = keep.tile([P, S // GROUP], U16, name="place")
-        tab_words = keep.tile([P, T], I32, name="tab_words", align_bytes=64)
-        tab_scales = keep.tile([P, T], U8, name="tab_scales", align_bytes=64)
+        tab_scales = keep.tile([P, T], U8, name="tab_scales", tag="scales_then_w1", align_bytes=64)
         w1_raw = keep.tile([P, PACK, 512], F32, name="w1_raw", tag="w1_raw_then_wgo", align_bytes=64)
         w2_plane = keep.tile([P, M], U8, name="w2_plane", align_bytes=64)
-        warm_in = keep.tile([P, 1], F32, name="warm_in")
-        warm_out = keep.tile([P, 1], F32, name="warm_out")
+        warm_in = keep.tile([P, 1], F32, name="warm_in", tag="warm_then_table", align_bytes=64)
+        warm_out = keep.tile([P, 1], F32, name="warm_out", tag="warm_then_w2", align_bytes=64)
         page_a = keep.tile([P, T], F32, name="page_a", align_bytes=64)
 
-        nc.vector.memset(tab_scales[:].bitcast(I32), 0)
-        nc.vector.memset(warm_in[:], 0.0)
-        nc.vector.memset(w2_plane[:].bitcast(I32), 0)
-        nc.vector.memset(page_a[:], 0.0)
+        page_b = keep.tile([P, T], F32, name="page_b", align_bytes=64)
+
+        nc.gpsimd.memset(warm_in[:], 0.0)
+        nc.gpsimd.memset(tab_scales[:].bitcast(I32), 0)
+        nc.gpsimd.memset(page_b[:], 0.0)
+        nc.gpsimd.memset(w2_plane[:].bitcast(I32), 0)
+        nc.vector.memset(page_a[:, 0 : T // 2 + 1], 0.0)
+        nc.vector.memset(page_a[:, T // 2 + 1 : T], 0.0)
+        nc.scalar.activation(warm_out[:], warm_in[:], RELU)
 
         nc.sync.dma_start(pick[:], offs)
         nc.sync.dma_start(w1_raw[:], w1.rearrange("(p j) c -> p j c", j=PACK))
-        nc.sync.dma_start(tab_words[:], tab[0, 0 : K * T].rearrange("(p b) -> p b", p=P).bitcast(I32))
         nc.sync.dma_start(place[:], offs2)
         scale_rows = tab[0, K * T : K * T + 16 * T].rearrange("(q b) -> q b", q=16).bitcast(I32)
         for q in range(4):
-            nc.scalar.dma_start(tab_scales[32 * q : 32 * q + 4, :].bitcast(I32), scale_rows[4 * q : 4 * q + 4, :])
-        nc.scalar.activation(warm_out[:], warm_in[:], RELU)
+            nc.sync.dma_start(tab_scales[32 * q : 32 * q + 4, :].bitcast(I32), scale_rows[4 * q : 4 * q + 4, :])
+        tab_words = keep.tile([P, T], I32, name="tab_words", tag="warm_then_table", align_bytes=64)
+        nc.sync.dma_start(tab_words[:], tab[0, 0 : K * T].rearrange("(p b) -> p b", p=P).bitcast(I32))
+        w2_codes = keep.tile([P, 2 * M], U8, name="w2_codes", tag="warm_then_w2", align_bytes=64)
+        nc.sync.dma_start(w2_codes[:].bitcast(I32), w2_words[0].bitcast(I32))
         w2_rows = w2_scales[0].bitcast(I32)
         for q in range(4):
             nc.sync.dma_start(w2_plane[32 * q : 32 * q + 4, :].bitcast(I32), w2_rows[4 * q : 4 * q + 4, :])
@@ -67,19 +73,17 @@ def tile_list_tabhs_m_none_kernel(tc, tab, w1, w2_words, w2_scales, wgo, offs, o
         v_scales = keep.tile([P, S], U8, name="v_scales", align_bytes=64)
         nc.vector.tensor_copy(v_scales[:], tab_scales[:].indirect(pick[:]))
 
-        w1_bf = keep.tile([P, 512 * PACK], BF16, name="w1_bf", tag="w1_bf_then_w2", align_bytes=64)
+        w1_bf = keep.tile([P, 512 * PACK], BF16, name="w1_bf", align_bytes=64)
         nc.scalar.copy(
             w1_bf[:].rearrange("p (t m j) -> p m j t", t=PACK, j=PACK),
             w1_raw[:].rearrange("p j (m t) -> p m j t", t=PACK),
         )
-        w1_codes = keep.tile([P, 512], U32, name="w1_codes", align_bytes=64)
+        w1_codes = keep.tile([P, 512], U32, name="w1_codes", tag="scales_then_w1", align_bytes=64)
         w1_plane = keep.tile([P, 512], U8, name="w1_plane", align_bytes=64)
         nc.vector.quantize_mx(out=w1_codes[:].bitcast(FP8X4), scales=w1_plane[:], in_=w1_bf[:])
 
         gate = keep.tile([P, S], F32, name="gate", tag="w1_raw_then_wgo", align_bytes=64)
         nc.sync.dma_start(gate[:], wgo)
-        w2_codes = keep.tile([P, 2 * M], U8, name="w2_codes", tag="w1_bf_then_w2", align_bytes=64)
-        nc.sync.dma_start(w2_codes[:].bitcast(I32), w2_words[0].bitcast(I32))
 
         v_words = keep.tile([P, S], U32, name="v_words", align_bytes=64)
         for j0, n in zip(starts(GATHERS), GATHERS):
@@ -88,7 +92,7 @@ def tile_list_tabhs_m_none_kernel(tc, tab, w1, w2_words, w2_scales, wgo, offs, o
                 tab_words[:].bitcast(U32).indirect(pick[:, j0 // GROUP : (j0 + n) // GROUP]),
             )
 
-        h_bf = keep.tile([P, S * PACK], BF16, name="h_bf", tag="h_bf_then_page", align_bytes=64)
+        h_bf = keep.tile([P, S * PACK], BF16, name="h_bf", align_bytes=64)
         h_codes = keep.tile([P, S], U32, name="h_codes", align_bytes=64)
         h_plane = keep.tile([P, S], U8, name="h_plane", align_bytes=64)
 
@@ -147,8 +151,6 @@ def tile_list_tabhs_m_none_kernel(tc, tab, w1, w2_words, w2_scales, wgo, offs, o
                 scatter(page_a, y0, *pieces[i - AHEAD])
         nc.sync.dma_start(out[0:P, :], page_a[:])
 
-        page_b = keep.tile([P, T], F32, name="page_b", tag="h_bf_then_page", align_bytes=64)
-        nc.gpsimd.memset(page_b[:], 0.0)
         for m in range(1, M // P):
             page = page_b if m % 2 else page_a
             y = ypool.tile([P, S], F32, name="y")

@@ -2,8 +2,8 @@ from contextlib import ExitStack
 
 import concourse.mybir as mybir
 
-K, M, T, S = 512, 512, 4096, 2048
-FLOPS = 2 * S * (K * 512 + 512 * M)
+K, H, M, T, S = 512, 512, 512, 4096, 2048
+FLOPS = 2 * S * (K * H + H * M)
 
 F32 = mybir.dt.float32
 BF16 = mybir.dt.bfloat16
@@ -20,92 +20,96 @@ P = 128
 PACK = 4
 GROUP = 16
 BANK = 512
-GATHERS = [512,512,1024]
-PIECES = [256,256,256,256,256,256,512]
-AHEAD = 2
-
-
-def starts(widths):
-    return [sum(widths[:i]) for i in range(len(widths))]
+PIECES = [256,256,512,512,512]
+VECTOR_ZEROES = 2944
 
 
 def tile_list_tabhs_m_none_kernel(tc, tab, w1, w2_words, w2_scales, wgo, offs, offs2, out):
     nc = tc.nc
     with ExitStack() as ctx:
         keep = ctx.enter_context(tc.tile_pool(name="keep", bufs=1))
-        ypool = ctx.enter_context(tc.tile_pool(name="ypool", bufs=2))
+        ypool = ctx.enter_context(tc.tile_pool(name="ypool", bufs=3))
         hpsum = ctx.enter_context(tc.psum_pool(name="hpsum", bufs=5))
         ypsum = ctx.enter_context(tc.psum_pool(name="ypsum", bufs=3))
 
+        def held(name, shape, dtype, tag=None):
+            return keep.tile(shape, dtype, name=name, tag=tag or name, align_bytes=64)
+
         pick = keep.tile([P, S // GROUP], U16, name="pick")
         place = keep.tile([P, S // GROUP], U16, name="place")
-        tab_scales = keep.tile([P, T], U8, name="tab_scales", tag="scales_then_w1", align_bytes=64)
-        w1_raw = keep.tile([P, PACK, 512], F32, name="w1_raw", tag="w1_raw_then_wgo", align_bytes=64)
-        w2_plane = keep.tile([P, M], U8, name="w2_plane", align_bytes=64)
-        warm_in = keep.tile([P, 1], F32, name="warm_in", tag="warm_then_table", align_bytes=64)
-        warm_out = keep.tile([P, 1], F32, name="warm_out", tag="warm_then_w2", align_bytes=64)
-        page_a = keep.tile([P, T], F32, name="page_a", align_bytes=64)
-
-        page_b = keep.tile([P, T], F32, name="page_b", align_bytes=64)
+        tab_scales = held("tab_scales", [P, T], U8, "scales_then_w1_codes")
+        w1_raw = held("w1_raw", [P, PACK, H], F32, "w1_then_wgo")
+        w2_plane = held("w2_plane", [P, M], U8)
+        warm_in = held("warm_in", [P, 1], F32, "warm_then_table")
+        warm_out = held("warm_out", [P, 1], F32, "warm_then_w2")
+        page_a = held("page_a", [P, T], F32)
+        page_b = held("page_b", [P, T], F32)
 
         nc.gpsimd.memset(warm_in[:], 0.0)
         nc.gpsimd.memset(tab_scales[:].bitcast(I32), 0)
-        nc.gpsimd.memset(page_b[:], 0.0)
+        nc.gpsimd.memset(page_a[:, VECTOR_ZEROES:T], 0.0)
         nc.gpsimd.memset(w2_plane[:].bitcast(I32), 0)
-        nc.vector.memset(page_a[:, 0 : T // 2 + 1], 0.0)
-        nc.vector.memset(page_a[:, T // 2 + 1 : T], 0.0)
+        nc.gpsimd.memset(page_b[:], 0.0)
+        nc.vector.memset(page_a[:, 0 : VECTOR_ZEROES // 2 + 1], 0.0)
+        nc.vector.memset(page_a[:, VECTOR_ZEROES // 2 + 1 : VECTOR_ZEROES], 0.0)
         nc.scalar.activation(warm_out[:], warm_in[:], RELU)
 
+        w1_rows = w1.rearrange("(p j) c -> p j c", j=PACK)
         nc.sync.dma_start(pick[:], offs)
-        nc.sync.dma_start(w1_raw[:], w1.rearrange("(p j) c -> p j c", j=PACK))
+        nc.sync.dma_start(w1_raw[:, 0:2, :], w1_rows[:, 0:2, :])
         nc.sync.dma_start(place[:], offs2)
         scale_rows = tab[0, K * T : K * T + 16 * T].rearrange("(q b) -> q b", q=16).bitcast(I32)
         for q in range(4):
             nc.sync.dma_start(tab_scales[32 * q : 32 * q + 4, :].bitcast(I32), scale_rows[4 * q : 4 * q + 4, :])
-        tab_words = keep.tile([P, T], I32, name="tab_words", tag="warm_then_table", align_bytes=64)
+        nc.sync.dma_start(w1_raw[:, 2:4, :], w1_rows[:, 2:4, :])
+        tab_words = held("tab_words", [P, T], I32, "warm_then_table")
         nc.sync.dma_start(tab_words[:], tab[0, 0 : K * T].rearrange("(p b) -> p b", p=P).bitcast(I32))
-        w2_codes = keep.tile([P, 2 * M], U8, name="w2_codes", tag="warm_then_w2", align_bytes=64)
+        w2_codes = held("w2_codes", [P, 2 * M], U8, "warm_then_w2")
         nc.sync.dma_start(w2_codes[:].bitcast(I32), w2_words[0].bitcast(I32))
         w2_rows = w2_scales[0].bitcast(I32)
         for q in range(4):
             nc.sync.dma_start(w2_plane[32 * q : 32 * q + 4, :].bitcast(I32), w2_rows[4 * q : 4 * q + 4, :])
 
-        v_scales = keep.tile([P, S], U8, name="v_scales", align_bytes=64)
-        nc.vector.tensor_copy(v_scales[:], tab_scales[:].indirect(pick[:]))
+        v_plane = held("v_plane", [P, S], U8)
+        nc.vector.tensor_copy(v_plane[:], tab_scales[:].indirect(pick[:]))
 
-        w1_bf = keep.tile([P, 512 * PACK], BF16, name="w1_bf", align_bytes=64)
+        w1_bf = held("w1_bf", [P, H * PACK], BF16)
         nc.scalar.copy(
             w1_bf[:].rearrange("p (t m j) -> p m j t", t=PACK, j=PACK),
             w1_raw[:].rearrange("p j (m t) -> p m j t", t=PACK),
         )
-        w1_codes = keep.tile([P, 512], U32, name="w1_codes", tag="scales_then_w1", align_bytes=64)
-        w1_plane = keep.tile([P, 512], U8, name="w1_plane", align_bytes=64)
+        w1_codes = held("w1_codes", [P, H], U32, "scales_then_w1_codes")
+        w1_plane = held("w1_plane", [P, H], U8)
         nc.vector.quantize_mx(out=w1_codes[:].bitcast(FP8X4), scales=w1_plane[:], in_=w1_bf[:])
 
-        gate = keep.tile([P, S], F32, name="gate", tag="w1_raw_then_wgo", align_bytes=64)
+        gate = held("gate", [P, S], F32, "w1_then_wgo")
         nc.sync.dma_start(gate[:], wgo)
 
-        v_words = keep.tile([P, S], U32, name="v_words", align_bytes=64)
-        for j0, n in zip(starts(GATHERS), GATHERS):
+        v_words = []
+
+        def gather(tag=None):
+            g = len(v_words)
+            v_words.append(held("v_words_%d" % g, [P, BANK], U32, tag))
             nc.vector.tensor_copy(
-                v_words[:, j0 : j0 + n],
-                tab_words[:].bitcast(U32).indirect(pick[:, j0 // GROUP : (j0 + n) // GROUP]),
+                v_words[g][:],
+                tab_words[:].bitcast(U32).indirect(pick[:, g * BANK // GROUP : (g + 1) * BANK // GROUP]),
             )
 
-        h_bf = keep.tile([P, S * PACK], BF16, name="h_bf", align_bytes=64)
-        h_codes = keep.tile([P, S], U32, name="h_codes", align_bytes=64)
-        h_plane = keep.tile([P, S], U8, name="h_plane", align_bytes=64)
+        h_codes = held("h_codes", [P, S], U32)
+        h_plane = held("h_plane", [P, S], U8)
 
         def hidden(j0, n):
-            for c0 in range(j0, j0 + n, P):
+            h_bf = held("h_bf_%d" % j0, [P, n * PACK], BF16)
+            for c0 in range(0, n, P):
+                g, v0 = divmod(j0 + c0, BANK)
                 bank = hpsum.tile([P, PACK, P], F32, name="h_bank")
                 for t in range(PACK):
                     nc.tensor.matmul_mx(
                         out=bank[:, t, :],
                         lhsT=w1_codes[:, t * P : (t + 1) * P].bitcast(FP8X4),
                         lhsT_scale=w1_plane[:, t * P : (t + 1) * P],
-                        rhs=v_words[:, c0 : c0 + P].bitcast(FP8X4),
-                        rhs_scale=v_scales[:, c0 : c0 + P],
+                        rhs=v_words[g][:, v0 : v0 + P].bitcast(FP8X4),
+                        rhs_scale=v_plane[:, j0 + c0 : j0 + c0 + P],
                         start=True,
                         stop=True,
                     )
@@ -117,7 +121,7 @@ def tile_list_tabhs_m_none_kernel(tc, tab, w1, w2_words, w2_scales, wgo, offs, o
             nc.vector.quantize_mx(
                 out=h_codes[:, j0 : j0 + n].bitcast(FP8X4),
                 scales=h_plane[:, j0 : j0 + n],
-                in_=h_bf[:, j0 * PACK : (j0 + n) * PACK],
+                in_=h_bf[:],
             )
 
         def project(m, y, j0, n):
@@ -141,18 +145,25 @@ def tile_list_tabhs_m_none_kernel(tc, tab, w1, w2_words, w2_scales, wgo, offs, o
                 MULT,
             )
 
-        pieces = list(zip(starts(PIECES), PIECES))
-        y0 = ypool.tile([P, S], F32, name="y")
-        for i in range(len(pieces) + AHEAD):
-            if i < len(pieces):
-                hidden(*pieces[i])
-            if i >= AHEAD:
-                project(0, y0, *pieces[i - AHEAD])
-                scatter(page_a, y0, *pieces[i - AHEAD])
+        pieces = [(sum(PIECES[:i]), n) for i, n in enumerate(PIECES)]
+        y_a = ypool.tile([P, S], F32, name="y")
+        y_b = ypool.tile([P, S], F32, name="y")
+        for g in range(S // BANK - 1):
+            gather()
+        hidden(*pieces[0])
+        gather("h_bf_0")
+        for i, piece in enumerate(pieces):
+            if i + 1 < len(pieces):
+                hidden(*pieces[i + 1])
+            for m, page, y in ((0, page_a, y_a), (1, page_b, y_b)):
+                project(m, y, *piece)
+                scatter(page, y, *piece)
         nc.sync.dma_start(out[0:P, :], page_a[:])
+        nc.sync.dma_start(out[P : 2 * P, :], page_b[:])
 
-        for m in range(1, M // P):
-            page = page_b if m % 2 else page_a
+        page_c = held("page_c", [P, T], F32, "h_bf_%d" % pieces[-1][0])
+        nc.gpsimd.memset(page_c[:], 0.0)
+        for m, page in ((2, page_c), (3, page_a)):
             y = ypool.tile([P, S], F32, name="y")
             for j0 in range(0, S, BANK):
                 project(m, y, j0, BANK)

@@ -21,7 +21,7 @@ PACK = 4
 GROUP = 16
 BANK = 512
 PIECES = [256,256,512,512,512]
-VECTOR_ZEROES = 2944
+VECTOR_ZEROES = 2816
 
 
 def tile_list_tabhs_m_none_kernel(tc, tab, w1, w2_words, w2_scales, wgo, offs, offs2, out):
@@ -40,16 +40,18 @@ def tile_list_tabhs_m_none_kernel(tc, tab, w1, w2_words, w2_scales, wgo, offs, o
         tab_scales = held("tab_scales", [P, T], U8, "scales_then_w1_codes")
         w1_raw = held("w1_raw", [P, PACK, H], F32, "w1_then_wgo")
         w2_plane = held("w2_plane", [P, M], U8)
-        warm_in = held("warm_in", [P, 1], F32, "warm_then_table")
-        warm_out = held("warm_out", [P, 1], F32, "warm_then_w2")
+        warm_in = held("warm_in", [P, 1], F32)
+        warm_out = held("warm_out", [P, 1], F32)
         page_a = held("page_a", [P, T], F32)
         page_b = held("page_b", [P, T], F32)
 
         nc.gpsimd.memset(warm_in[:], 0.0)
         nc.gpsimd.memset(tab_scales[:].bitcast(I32), 0)
+        v_plane = held("v_plane", [P, S], U8)
+        nc.gpsimd.memset(v_plane[:].bitcast(I32), 0)
         nc.gpsimd.memset(page_a[:, VECTOR_ZEROES:T], 0.0)
-        nc.gpsimd.memset(w2_plane[:].bitcast(I32), 0)
         nc.gpsimd.memset(page_b[:], 0.0)
+        nc.gpsimd.memset(w2_plane[:].bitcast(I32), 0)
         nc.vector.memset(page_a[:, 0 : VECTOR_ZEROES // 2 + 1], 0.0)
         nc.vector.memset(page_a[:, VECTOR_ZEROES // 2 + 1 : VECTOR_ZEROES], 0.0)
         nc.scalar.activation(warm_out[:], warm_in[:], RELU)
@@ -59,19 +61,22 @@ def tile_list_tabhs_m_none_kernel(tc, tab, w1, w2_words, w2_scales, wgo, offs, o
         nc.sync.dma_start(w1_raw[:, 0:2, :], w1_rows[:, 0:2, :])
         nc.sync.dma_start(place[:], offs2)
         scale_rows = tab[0, K * T : K * T + 16 * T].rearrange("(q b) -> q b", q=16).bitcast(I32)
-        for q in range(4):
-            nc.sync.dma_start(tab_scales[32 * q : 32 * q + 4, :].bitcast(I32), scale_rows[4 * q : 4 * q + 4, :])
+        nc.sync.dma_start(tab_scales[0:P:8, :].bitcast(I32), scale_rows)
         nc.sync.dma_start(w1_raw[:, 2:4, :], w1_rows[:, 2:4, :])
-        tab_words = held("tab_words", [P, T], I32, "warm_then_table")
+        tab_words = held("tab_words", [P, T], I32)
         nc.sync.dma_start(tab_words[:], tab[0, 0 : K * T].rearrange("(p b) -> p b", p=P).bitcast(I32))
-        w2_codes = held("w2_codes", [P, 2 * M], U8, "warm_then_w2")
+        w2_codes = held("w2_codes", [P, 2 * M], U8)
         nc.sync.dma_start(w2_codes[:].bitcast(I32), w2_words[0].bitcast(I32))
+
+        for j0, j1 in ((0, S // 2), (S // 2, S)):
+            picked = held("picked_%d" % j0, [P, j1 - j0], U8)
+            nc.vector.tensor_copy(picked[:], tab_scales[:].indirect(pick[:, j0 // GROUP : j1 // GROUP]))
+            for r in range(4):
+                nc.sync.dma_start(v_plane[r:P:32, j0:j1].bitcast(I32), picked[8 * r : P : 32, :].bitcast(I32))
+
         w2_rows = w2_scales[0].bitcast(I32)
         for q in range(4):
-            nc.sync.dma_start(w2_plane[32 * q : 32 * q + 4, :].bitcast(I32), w2_rows[4 * q : 4 * q + 4, :])
-
-        v_plane = held("v_plane", [P, S], U8)
-        nc.vector.tensor_copy(v_plane[:], tab_scales[:].indirect(pick[:]))
+            nc.gpsimd.dma_start(w2_plane[32 * q : 32 * q + 4, :].bitcast(I32), w2_rows[4 * q : 4 * q + 4, :])
 
         w1_bf = held("w1_bf", [P, H * PACK], BF16)
         nc.scalar.copy(

from contextlib import ExitStack

import concourse.mybir as mybir

K, H, M, T, S = 512, 512, 512, 4096, 2048
FLOPS = 2 * S * (K * H + H * M)

F32 = mybir.dt.float32
BF16 = mybir.dt.bfloat16
I32 = mybir.dt.int32
U32 = mybir.dt.uint32
U16 = mybir.dt.uint16
U8 = mybir.dt.uint8
FP8X4 = mybir.dt.float8_e4m3fn_x4
FP4X4 = mybir.dt.float4_e2m1fn_x4
RELU = mybir.ActivationFunctionType.Relu
MULT = mybir.AluOpType.mult

P = 128
PACK = 4
GROUP = 16
BANK = 512
PIECES = [256,256,512,512,512]
VECTOR_ZEROES = 2816


def tile_list_tabhs_m_none_kernel(tc, tab, w1, w2_words, w2_scales, wgo, offs, offs2, out):
    nc = tc.nc
    with ExitStack() as ctx:
        keep = ctx.enter_context(tc.tile_pool(name="keep", bufs=1))
        ypool = ctx.enter_context(tc.tile_pool(name="ypool", bufs=3))
        hpsum = ctx.enter_context(tc.psum_pool(name="hpsum", bufs=5))
        ypsum = ctx.enter_context(tc.psum_pool(name="ypsum", bufs=3))

        def held(name, shape, dtype, tag=None):
            return keep.tile(shape, dtype, name=name, tag=tag or name, align_bytes=64)

        pick = keep.tile([P, S // GROUP], U16, name="pick")
        place = keep.tile([P, S // GROUP], U16, name="place")
        tab_scales = held("tab_scales", [P, T], U8, "scales_then_w1_codes")
        w1_raw = held("w1_raw", [P, PACK, H], F32, "w1_then_wgo")
        w2_plane = held("w2_plane", [P, M], U8)
        warm_in = held("warm_in", [P, 1], F32)
        warm_out = held("warm_out", [P, 1], F32)
        page_a = held("page_a", [P, T], F32)
        page_b = held("page_b", [P, T], F32)

        nc.gpsimd.memset(warm_in[:], 0.0)
        nc.gpsimd.memset(tab_scales[:].bitcast(I32), 0)
        v_plane = held("v_plane", [P, S], U8)
        nc.gpsimd.memset(v_plane[:].bitcast(I32), 0)
        nc.gpsimd.memset(page_a[:, VECTOR_ZEROES:T], 0.0)
        nc.gpsimd.memset(page_b[:], 0.0)
        nc.gpsimd.memset(w2_plane[:].bitcast(I32), 0)
        nc.vector.memset(page_a[:, 0 : VECTOR_ZEROES // 2 + 1], 0.0)
        nc.vector.memset(page_a[:, VECTOR_ZEROES // 2 + 1 : VECTOR_ZEROES], 0.0)
        nc.scalar.activation(warm_out[:], warm_in[:], RELU)

        w1_rows = w1.rearrange("(p j) c -> p j c", j=PACK)
        nc.sync.dma_start(pick[:], offs)
        nc.sync.dma_start(w1_raw[:, 0:2, :], w1_rows[:, 0:2, :])
        nc.sync.dma_start(place[:], offs2)
        scale_rows = tab[0, K * T : K * T + 16 * T].rearrange("(q b) -> q b", q=16).bitcast(I32)
        nc.sync.dma_start(tab_scales[0:P:8, :].bitcast(I32), scale_rows)
        nc.sync.dma_start(w1_raw[:, 2:4, :], w1_rows[:, 2:4, :])
        tab_words = held("tab_words", [P, T], I32)
        nc.sync.dma_start(tab_words[:], tab[0, 0 : K * T].rearrange("(p b) -> p b", p=P).bitcast(I32))
        w2_codes = held("w2_codes", [P, 2 * M], U8)
        nc.sync.dma_start(w2_codes[:].bitcast(I32), w2_words[0].bitcast(I32))

        for j0, j1 in ((0, S // 2), (S // 2, S)):
            picked = held("picked_%d" % j0, [P, j1 - j0], U8)
            nc.vector.tensor_copy(picked[:], tab_scales[:].indirect(pick[:, j0 // GROUP : j1 // GROUP]))
            for r in range(4):
                nc.sync.dma_start(v_plane[r:P:32, j0:j1].bitcast(I32), picked[8 * r : P : 32, :].bitcast(I32))

        w2_rows = w2_scales[0].bitcast(I32)
        for q in range(4):
            nc.gpsimd.dma_start(w2_plane[32 * q : 32 * q + 4, :].bitcast(I32), w2_rows[4 * q : 4 * q + 4, :])

        w1_bf = held("w1_bf", [P, H * PACK], BF16)
        nc.scalar.copy(
            w1_bf[:].rearrange("p (t m j) -> p m j t", t=PACK, j=PACK),
            w1_raw[:].rearrange("p j (m t) -> p m j t", t=PACK),
        )
        w1_codes = held("w1_codes", [P, H], U32, "scales_then_w1_codes")
        w1_plane = held("w1_plane", [P, H], U8)
        nc.vector.quantize_mx(out=w1_codes[:].bitcast(FP8X4), scales=w1_plane[:], in_=w1_bf[:])

        gate = held("gate", [P, S], F32, "w1_then_wgo")
        nc.sync.dma_start(gate[:], wgo)

        v_words = []

        def gather(tag=None):
            g = len(v_words)
            v_words.append(held("v_words_%d" % g, [P, BANK], U32, tag))
            nc.vector.tensor_copy(
                v_words[g][:],
                tab_words[:].bitcast(U32).indirect(pick[:, g * BANK // GROUP : (g + 1) * BANK // GROUP]),
            )

        h_codes = held("h_codes", [P, S], U32)
        h_plane = held("h_plane", [P, S], U8)

        def hidden(j0, n):
            h_bf = held("h_bf_%d" % j0, [P, n * PACK], BF16)
            for c0 in range(0, n, P):
                g, v0 = divmod(j0 + c0, BANK)
                bank = hpsum.tile([P, PACK, P], F32, name="h_bank")
                for t in range(PACK):
                    nc.tensor.matmul_mx(
                        out=bank[:, t, :],
                        lhsT=w1_codes[:, t * P : (t + 1) * P].bitcast(FP8X4),
                        lhsT_scale=w1_plane[:, t * P : (t + 1) * P],
                        rhs=v_words[g][:, v0 : v0 + P].bitcast(FP8X4),
                        rhs_scale=v_plane[:, j0 + c0 : j0 + c0 + P],
                        start=True,
                        stop=True,
                    )
                nc.scalar.activation(
                    h_bf[:, c0 * PACK : (c0 + P) * PACK].rearrange("p (n t) -> p n t", t=PACK),
                    bank[:].rearrange("p t n -> p n t"),
                    RELU,
                )
            nc.vector.quantize_mx(
                out=h_codes[:, j0 : j0 + n].bitcast(FP8X4),
                scales=h_plane[:, j0 : j0 + n],
                in_=h_bf[:],
            )

        def project(m, y, j0, n):
            bank = ypsum.tile([P, BANK], F32, name="y_bank")
            nc.tensor.matmul_mx(
                out=bank[:, 0:n],
                lhsT=w2_codes[:, 2 * m * P : 2 * (m + 1) * P].bitcast(FP4X4),
                lhsT_scale=w2_plane[:, m * P : (m + 1) * P],
                rhs=h_codes[:, j0 : j0 + n].bitcast(FP8X4),
                rhs_scale=h_plane[:, j0 : j0 + n],
                start=True,
                stop=True,
            )
            nc.scalar.copy(y[:, j0 : j0 + n], bank[:, 0:n])

        def scatter(page, y, j0, n):
            nc.vector.tensor_tensor(
                page[:].indirect(place[:, j0 // GROUP : (j0 + n) // GROUP]),
                y[:, j0 : j0 + n],
                gate[:, j0 : j0 + n],
                MULT,
            )

        pieces = [(sum(PIECES[:i]), n) for i, n in enumerate(PIECES)]
        y_a = ypool.tile([P, S], F32, name="y")
        y_b = ypool.tile([P, S], F32, name="y")
        for g in range(S // BANK - 1):
            gather()
        hidden(*pieces[0])
        gather("h_bf_0")
        for i, piece in enumerate(pieces):
            if i + 1 < len(pieces):
                hidden(*pieces[i + 1])
            for m, page, y in ((0, page_a, y_a), (1, page_b, y_b)):
                project(m, y, *piece)
                scatter(page, y, *piece)
        nc.sync.dma_start(out[0:P, :], page_a[:])
        nc.sync.dma_start(out[P : 2 * P, :], page_b[:])

        page_c = held("page_c", [P, T], F32, "h_bf_%d" % pieces[-1][0])
        nc.gpsimd.memset(page_c[:], 0.0)
        for m, page in ((2, page_c), (3, page_a)):
            y = ypool.tile([P, S], F32, name="y")
            for j0 in range(0, S, BANK):
                project(m, y, j0, BANK)
            scatter(page, y, 0, S)
            nc.sync.dma_start(out[m * P : (m + 1) * P, :], page[:])
